import numpy as np
import ml_dtypes


def mxq(x, axis, fmt="e4m3"):
    dtype, down = {"e4m3": (ml_dtypes.float8_e4m3fn, 7), "e5m2": (ml_dtypes.float8_e5m2, 14)}[fmt]
    v = np.moveaxis(np.asarray(x, np.float32).astype(ml_dtypes.bfloat16).astype(np.float64), axis, -1)
    blocks = v.reshape(v.shape[:-1] + (-1, 32))
    amax = np.abs(blocks).max(-1, keepdims=True)
    byte = np.maximum(np.where(amax > 0, np.frexp(amax)[1] - 1 + 127, 0) - down, 1)
    scale = np.exp2(byte - 127.0)
    codes = (blocks / scale).astype(np.float32).astype(dtype).astype(np.float64)
    return np.moveaxis((codes * scale).reshape(v.shape), -1, axis)


WIDE = False


def mx_kscale(k):
    if not WIDE:
        return np.ones(k)
    levels = np.array([10, -10, 5, -5, 0])
    if k % 512:
        return np.exp2(np.random.permutation(np.resize(levels, k // 32))).repeat(32)
    a = np.empty((k // 512, 16))
    for p in range(k // 512):
        a[p, :8] = np.random.permutation(np.resize(levels, 8))
        for g in range(8):
            far = levels[np.abs(levels - a[p, g]) >= 10]
            a[p, g + 8] = far[np.random.randint(len(far))]
    return np.exp2(a.ravel()).repeat(32)


def f64(x):
    return np.asarray(x).astype(np.float64)


def striped(idx):
    return np.tile(idx.reshape(-1, 16).T, (8, 1)).astype(np.uint16)


def unstriped(offs):
    return offs[:16].T.reshape(-1).astype(np.int64)


def striped8(idx):
    return np.concatenate([x.reshape(-1, 16).T for x in idx]).astype(np.uint16)


def runs(offs, k):
    lists = np.stack([offs[16 * r : 16 * r + 16].T.reshape(-1) for r in range(8)]).astype(np.int64)
    return lists[np.arange(k) % 512 // 64]


def pack_weight(w):
    k, n = w.shape
    w = f64(np.asarray(w, np.float32).astype(ml_dtypes.bfloat16)).reshape(k // 32, 32, n)
    amax = np.abs(w).max(1)
    byte = np.clip(np.where(amax > 0, np.frexp(amax)[1] - 1 + 127 - 7, 1), 1, 254)
    scaled = (w * np.exp2(127.0 - byte)[:, None, :]).reshape(k, n).astype(np.float32)
    words = np.ascontiguousarray(scaled.reshape(k // 512, 128, 4, n).transpose(0, 1, 3, 2)).astype(ml_dtypes.float8_e4m3fn).view(np.uint8)
    return words, np.ascontiguousarray(byte.astype(np.uint8).reshape(k // 512, 16, n))


def unpack_weight(words, scales):
    g, p, n, _ = words.shape
    vals = np.ascontiguousarray(words).view(ml_dtypes.float8_e4m3fn).astype(np.float64) * np.repeat(np.exp2(scales.astype(np.float64) - 127.0), 8, axis=1)[..., None]
    return vals.transpose(0, 1, 3, 2).reshape(g * 512, n)


def relu(v):
    return np.maximum(v, 0.0)


def sigmoid(v):
    return 1.0 / (1.0 + np.exp(-np.maximum(v, -700.0)))


K, T, S, V, H, C = 512, 2048, 1024, 512, 512, 512


def setup_inputs():
    n = np.random.standard_normal
    s = mx_kscale(K)[:, None]
    packed_xT = pack_weight(n((K, T)) * s)
    return {
        "x_words": packed_xT[0],
        "x_scales": packed_xT[1],
        "w1": (n((K, H)) / np.sqrt(K) / s).astype(np.float32),
        "gs": (np.random.uniform(0.5, 1.5, (K, 1)) / s).astype(np.float32),
        "offs": striped(np.random.permutation(T)[:S]),
        "n1": striped8(np.stack([np.random.permutation(S) for _ in range(8)])),
        "cand": striped(np.random.permutation(T)[:C]),
        "n2": striped8(np.stack([np.random.permutation(V) for _ in range(8)])),
    }


def reference(x_words, x_scales, w1, gs, offs, n1, cand, n2):
    x_cand = unpack_weight(x_words, x_scales)[:, unstriped(cand)]
    xq = unpack_weight(x_words, x_scales)[:, unstriped(offs)]
    y = mxq(f64(w1), 0, "e4m3").T @ xq
    ln = y[np.arange(H)[:, None], runs(n1, H)]
    mx = ln.reshape(H, V, 2).max(axis=2)
    mn = ln.reshape(H, V, 2).min(axis=2)
    z = f64(gs) * (mx * sigmoid(mn))
    s = 0.0625 * ((x_cand.T @ mxq(z, 0, "e4m3")))
    rl = relu(s)
    ds = np.zeros((C, V))
    ds[np.arange(C)[:, None], runs(n2, C)] = rl
    return ds - (0.5 * s)

@@ -1,0 +1,176 @@
+from contextlib import ExitStack
+
+import concourse.mybir as mybir
+
+K, T, S, V, H, C = 512, 2048, 1024, 512, 512, 512
+FLOPS = 2 * K * H * S + 2 * K * C * V
+
+F32 = mybir.dt.float32
+BF16 = mybir.dt.bfloat16
+I32 = mybir.dt.int32
+U32 = mybir.dt.uint32
+U16 = mybir.dt.uint16
+U8 = mybir.dt.uint8
+FP8X4 = mybir.dt.float8_e4m3fn_x4
+ACT = mybir.ActivationFunctionType
+ALU = mybir.AluOpType
+
+P = 128
+PACK = 4
+BANK = 512
+STRIPE = 16
+W_PIECES = ((0, 128), (128, 320), (320, 512))
+CHUNKS = (128, 128, 128, 128)
+
+
+def tile_picked_candpgatesend_none_p_kernel(tc, x_words, x_scales, w1, gs, offs, n1, cand, n2, out):
+    nc = tc.nc
+    with ExitStack() as ctx:
+        lists = ctx.enter_context(tc.tile_pool(name="lists", bufs=1))
+        keep = ctx.enter_context(tc.tile_pool(name="keep", bufs=1))
+        ring = ctx.enter_context(tc.tile_pool(name="ring", bufs=2))
+        psum = ctx.enter_context(tc.psum_pool(name="psum", bufs=1))
+
+        offs_sb = lists.tile([P, S // STRIPE], U16, name="offs_sb")
+        cand_sb = lists.tile([P, C // STRIPE], U16, name="cand_sb")
+        n1_sb = lists.tile([P, S // STRIPE], U16, name="n1_sb")
+        n2_sb = lists.tile([P, V // STRIPE], U16, name="n2_sb")
+
+        scale_table = keep.tile([P, T], U8, name="scale_table", align_bytes=64)
+        word_table = keep.tile([P, T], I32, name="word_table", align_bytes=64)
+        nc.vector.memset(scale_table[:].bitcast(I32), 0)
+
+        nc.sync.dma_start(offs_sb[:], offs)
+        nc.sync.dma_start(cand_sb[:], cand)
+        w_rows = w1.rearrange("(p j) c -> p j c", j=PACK)
+        w_raw = [keep.tile([P, PACK, hi - lo], F32, name=f"w_raw{lo}") for lo, hi in W_PIECES]
+        nc.sync.dma_start(w_raw[0][:], w_rows[:, :, W_PIECES[0][0] : W_PIECES[0][1]])
+        for q in range(4):
+            nc.sync.dma_start(scale_table[32 * q : 32 * q + 4, :].bitcast(I32), x_scales[0, 4 * q : 4 * q + 4, :].bitcast(I32))
+        for piece, (lo, hi) in list(zip(w_raw, W_PIECES))[1:]:
+            nc.sync.dma_start(piece[:], w_rows[:, :, lo:hi])
+        nc.sync.dma_start(word_table[:], x_words[0].rearrange("p n t -> p (n t)").bitcast(I32))
+        nc.sync.dma_start(n1_sb[:], n1)
+        gs_sb = keep.tile([P, PACK], F32, name="gs_sb")
+        nc.sync.dma_start(gs_sb[:], gs.rearrange("(p t) o -> p (t o)", t=PACK))
+        nc.sync.dma_start(n2_sb[:], n2)
+
+        xq_scales = keep.tile([P, S], U8, name="xq_scales", align_bytes=64)
+        nc.vector.tensor_copy(xq_scales[:], scale_table[:].indirect(offs_sb[:]))
+        xc_scales = keep.tile([P, C], U8, name="xc_scales", align_bytes=64)
+        nc.vector.tensor_copy(xc_scales[:].rearrange("p (t m) -> p m t", t=PACK), scale_table[:].indirect(cand_sb[:]))
+
+        w_grouped = keep.tile([P, PACK * H], BF16, name="w_grouped", tag="first", align_bytes=64)
+        w_dst = w_grouped[:].rearrange("p (t m j) -> p m t j", t=PACK, j=PACK)
+        for piece, (lo, hi) in zip(w_raw, W_PIECES):
+            nc.scalar.copy(w_dst[:, lo // PACK : hi // PACK], piece[:].rearrange("p j (m t) -> p m t j", t=PACK))
+        w_codes = keep.tile([P, H], U32, name="w_codes", align_bytes=64)
+        w_scales = keep.tile([P, H], U8, name="w_scales", align_bytes=64)
+        nc.vector.quantize_mx(out=w_codes[:].bitcast(FP8X4), scales=w_scales[:], in_=w_grouped[:])
+
+        xq_words = []
+        for h in range(S // BANK):
+            picked = keep.tile([P, BANK], U32, name=f"xq_words{h}", tag=("first", "second")[h], align_bytes=64)
+            nc.vector.tensor_copy(picked[:], word_table[:].bitcast(U32).indirect(offs_sb[:, h * BANK // STRIPE : (h + 1) * BANK // STRIPE]))
+            xq_words.append(picked)
+        xc_words = keep.tile([P, C], U32, name="xc_words", align_bytes=64)
+        nc.vector.tensor_copy(xc_words[:].rearrange("p (t m) -> p m t", t=PACK), word_table[:].bitcast(U32).indirect(cand_sb[:]))
+
+        y = [keep.tile([P, S], F32, name=f"y{t}") for t in range(PACK)]
+        for pair in range(2):
+            for h in range(S // BANK):
+                for t in (2 * pair, 2 * pair + 1):
+                    cols = slice(h * BANK, (h + 1) * BANK)
+                    rows = slice(t * P, (t + 1) * P)
+                    acc = psum.tile([P, BANK], F32, name=f"y_acc{h}{t}", tag=f"bank{h}{t}")
+                    nc.tensor.matmul_mx(out=acc[:], lhsT=w_codes[:, rows].bitcast(FP8X4), lhsT_scale=w_scales[:, rows],
+                                        rhs=xq_words[h][:].bitcast(FP8X4), rhs_scale=xq_scales[:, cols], start=True, stop=True)
+                    if pair == 1 and h == 0:
+                        nc.vector.tensor_copy(y[t][:, cols], acc[:])
+                    else:
+                        nc.scalar.copy(y[t][:, cols], acc[:])
+
+        score = [psum.tile([P, V], F32, name=f"score{t}", tag=f"bank0{t}") for t in range(PACK)]
+        ds = [keep.tile([P, V], F32, name=f"ds{t}") for t in range(PACK)]
+        out_rows = out.rearrange("(p t) v -> p t v", t=PACK)
+
+        def fetch(c, v0, n):
+            ln = keep.tile([P, PACK, 2 * n], F32, name="ln")
+            picks = n1_sb[:, 2 * v0 // STRIPE : 2 * (v0 + n) // STRIPE]
+            for t in range(PACK):
+                if c == 0 and t in (0, 2):
+                    nc.vector.tensor_copy(ln[:, t, :], y[t][:].indirect(picks))
+                else:
+                    nc.scalar.activation(ln[:, t, :], y[t][:].indirect(picks), ACT.Copy)
+            return ln
+
+        def gate(c, ln, n):
+            pairs = ln[:].rearrange("p t (v e) -> p (t v) e", e=2)
+            if c == 1:
+                both = keep.tile([P, 2, PACK * n], F32, name="both", tag="turn", align_bytes=64)
+                mn, mx = both[:, 0, :], both[:, 1, :]
+            else:
+                mn = keep.tile([P, PACK * n], F32, name="mn")[:]
+                mx = keep.tile([P, PACK * n], F32, name="mx", tag="turn", align_bytes=64)[:]
+            sg = ring.tile([P, PACK * n], F32, name="sg")
+            nc.vector.tensor_tensor(mn, pairs[:, :, 0], pairs[:, :, 1], ALU.min)
+            nc.vector.tensor_tensor(mx, pairs[:, :, 0], pairs[:, :, 1], ALU.max)
+            nc.scalar.activation(sg[:], mn, ACT.Sigmoid)
+            return mx, sg
+
+        def quantise(c, mx, sg, n):
+            if c == 0 or False:
+                z_rows = ring.tile([P, PACK, n], BF16, name="z_rows")
+                for t in range(PACK):
+                    part = slice(t * n, (t + 1) * n)
+                    nc.vector.scalar_tensor_tensor(z_rows[:, t, :], mx[:, part], gs_sb[:, t : t + 1], sg[:, part], ALU.mult, ALU.mult)
+                z_grouped = keep.tile([P, PACK * n], BF16, name="z_grouped", tag="turn", align_bytes=64)
+                if c == 0:
+                    nc.vector.tensor_copy(z_grouped[:].rearrange("p (v t) -> p v t", t=PACK), z_rows[:].rearrange("p t v -> p v t"))
+                else:
+                    nc.scalar.copy(z_grouped[:].rearrange("p (v t) -> p v t", t=PACK), z_rows[:].rearrange("p t v -> p v t"))
+            else:
+                gated = ring.tile([P, PACK * n], F32, name="gated")
+                nc.gpsimd.tensor_tensor(gated[:], mx, sg[:], ALU.mult)
+                z_grouped = keep.tile([P, PACK * n], BF16, name="z_grouped", tag="turn", align_bytes=64)
+                nc.gpsimd.tensor_tensor(z_grouped[:].rearrange("p (v t) -> p v t", t=PACK), gated[:].rearrange("p (t v) -> p v t", t=PACK),
+                                        gs_sb[:].unsqueeze(1).to_broadcast([P, n, PACK]), ALU.mult)
+            z_codes = ring.tile([P, n], U32, name="z_codes", align_bytes=64)
+            z_scales = ring.tile([P, n], U8, name="z_scales", align_bytes=64)
+            nc.vector.quantize_mx(out=z_codes[:].bitcast(FP8X4), scales=z_scales[:], in_=z_grouped[:])
+            return z_codes, z_scales
+
+        def multiply(z_codes, z_scales, v0, n):
+            rl = ring.tile([P, PACK, n], F32, name="rl")
+            for t in range(PACK):
+                rows = slice(t * P, (t + 1) * P)
+                nc.tensor.matmul_mx(out=score[t][:, v0 : v0 + n], lhsT=xc_words[:, rows].bitcast(FP8X4), lhsT_scale=xc_scales[:, rows],
+                                    rhs=z_codes[:].bitcast(FP8X4), rhs_scale=z_scales[:], start=True, stop=True)
+                nc.scalar.activation(rl[:, t, :], score[t][:, v0 : v0 + n], ACT.Relu, scale=0.0625)
+            return rl
+
+        def send(rl, v0, n, last):
+            places = n2_sb[:, v0 // STRIPE : (v0 + n) // STRIPE]
+            for t in range(PACK):
+                nc.vector.tensor_copy(ds[t][:].indirect(places), rl[:, t, :])
+                if last:
+                    result = keep.tile([P, V], F32, name=f"result{t}")
+                    if t < 2 and True:
+                        less = keep.tile([P, V], F32, name=f"less{t}")
+                        nc.scalar.activation(less[:], score[t][:], ACT.Copy, scale=-0.03125)
+                        nc.gpsimd.tensor_tensor(result[:], less[:], ds[t][:], ALU.add)
+                    else:
+                        nc.vector.scalar_tensor_tensor(result[:], score[t][:], -0.03125, ds[t][:], ALU.mult, ALU.add)
+                    nc.sync.dma_start(out_rows[:, t, :], result[:])
+
+        starts = [sum(CHUNKS[:c]) for c in range(len(CHUNKS))]
+        last = len(CHUNKS) - 1
+        fetched = fetch(0, starts[0], CHUNKS[0])
+        gated_pair = gate(0, fetched, CHUNKS[0])
+        for c, n in enumerate(CHUNKS):
+            codes = quantise(c, *gated_pair, n)
+            rl = multiply(*codes, starts[c], n)
+            if c < last:
+                fetched = fetch(c + 1, starts[c + 1], CHUNKS[c + 1])
+                gated_pair = gate(c + 1, fetched, CHUNKS[c + 1])
+            send(rl, starts[c], n, c == last)

@@ -39,6 +39,10 @@ def tile_picked_candpgatesend_none_p_kernel(tc, x_words, x_scales, w1, gs, offs,
         scale_table = keep.tile([P, T], U8, name="scale_table", align_bytes=64)
         word_table = keep.tile([P, T], I32, name="word_table", align_bytes=64)
         nc.vector.memset(scale_table[:].bitcast(I32), 0)
+        warm_in = keep.tile([P, 8], F32, name="warm_in")
+        warm_out = keep.tile([P, 8], F32, name="warm_out")
+        nc.gpsimd.memset(warm_in[:], 0.0)
+        nc.scalar.activation(warm_out[:], warm_in[:], ACT.Sigmoid)
 
         nc.sync.dma_start(offs_sb[:], offs)
         nc.sync.dma_start(cand_sb[:], cand)

@@ -20,6 +20,7 @@ PACK = 4
 BANK = 512
 STRIPE = 16
 W_PIECES = ((0, 128), (128, 320), (320, 512))
+HELD = ((1, 3), (2, 3))
 CHUNKS = (128, 128, 128, 128)
 
 
@@ -81,61 +82,66 @@ def tile_picked_candpgatesend_none_p_kernel(tc, x_words, x_scales, w1, gs, offs,
         nc.vector.tensor_copy(xc_words[:].rearrange("p (t m) -> p m t", t=PACK), word_table[:].bitcast(U32).indirect(cand_sb[:]))
 
         y = [keep.tile([P, S], F32, name=f"y{t}") for t in range(PACK)]
-        for pair in range(2):
+        starts = [sum(CHUNKS[:c]) for c in range(len(CHUNKS))]
+        last = len(CHUNKS) - 1
+
+        def project(pair):
             for h in range(S // BANK):
-                for t in (2 * pair, 2 * pair + 1):
+                for t in pair:
                     cols = slice(h * BANK, (h + 1) * BANK)
                     rows = slice(t * P, (t + 1) * P)
                     acc = psum.tile([P, BANK], F32, name=f"y_acc{h}{t}", tag=f"bank{h}{t}")
                     nc.tensor.matmul_mx(out=acc[:], lhsT=w_codes[:, rows].bitcast(FP8X4), lhsT_scale=w_scales[:, rows],
                                         rhs=xq_words[h][:].bitcast(FP8X4), rhs_scale=xq_scales[:, cols], start=True, stop=True)
-                    if pair == 1 and h == 0:
+                    if pair[0] == 2 and h == 0:
                         nc.vector.tensor_copy(y[t][:, cols], acc[:])
                     else:
                         nc.scalar.copy(y[t][:, cols], acc[:])
 
-        score = [psum.tile([P, V], F32, name=f"score{t}", tag=f"bank0{t}") for t in range(PACK)]
-        ds = [keep.tile([P, V], F32, name=f"ds{t}") for t in range(PACK)]
-        out_rows = out.rearrange("(p t) v -> p t v", t=PACK)
-
-        def fetch(c, v0, n):
-            ln = keep.tile([P, PACK, 2 * n], F32, name="ln")
+        def fetch(c, group):
+            v0, n = starts[c], CHUNKS[c]
+            ln = keep.tile([P, len(group), 2 * n], F32, name="ln", tag="mn" if c == 1 and group[0] == 0 else f"ln{group[-1]}")
             picks = n1_sb[:, 2 * v0 // STRIPE : 2 * (v0 + n) // STRIPE]
-            for t in range(PACK):
-                if c == 0 and t in (0, 2):
-                    nc.vector.tensor_copy(ln[:, t, :], y[t][:].indirect(picks))
+            for i, t in enumerate(group):
+                if c == 0 and i == 0:
+                    nc.vector.tensor_copy(ln[:, i, :], y[t][:].indirect(picks))
                 else:
-                    nc.scalar.activation(ln[:, t, :], y[t][:].indirect(picks), ACT.Copy)
+                    nc.scalar.activation(ln[:, i, :], y[t][:].indirect(picks), ACT.Copy)
             return ln
 
-        def gate(c, ln, n):
-            pairs = ln[:].rearrange("p t (v e) -> p (t v) e", e=2)
+        def gate_tiles(c):
+            n = CHUNKS[c]
             if c == 1:
-                both = keep.tile([P, 2, PACK * n], F32, name="both", tag="turn", align_bytes=64)
-                mn, mx = both[:, 0, :], both[:, 1, :]
+                both = keep.tile([P, 2 * PACK * n], F32, name="both", tag="turn", align_bytes=64)
+                mn, mx = both[:, : PACK * n], both[:, PACK * n :]
             else:
                 mn = keep.tile([P, PACK * n], F32, name="mn")[:]
                 mx = keep.tile([P, PACK * n], F32, name="mx", tag="turn", align_bytes=64)[:]
             sg = ring.tile([P, PACK * n], F32, name="sg")
-            nc.vector.tensor_tensor(mn, pairs[:, :, 0], pairs[:, :, 1], ALU.min)
-            nc.vector.tensor_tensor(mx, pairs[:, :, 0], pairs[:, :, 1], ALU.max)
-            nc.scalar.activation(sg[:], mn, ACT.Sigmoid)
-            return mx, sg
+            return mn, mx, sg[:]
 
-        def quantise(c, mx, sg, n):
-            if c == 0 or False:
-                z_rows = ring.tile([P, PACK, n], BF16, name="z_rows")
+        def gate(c, groups, fetched, mn, mx, sg):
+            n = CHUNKS[c]
+            parts = [slice(group[0] * n, (group[-1] + 1) * n) for group in groups]
+            pairs = [ln[:].rearrange("p t (v e) -> p (t v) e", e=2) for ln in fetched]
+            for part, pair in zip(parts, pairs):
+                nc.vector.tensor_tensor(mn[:, part], pair[:, :, 0], pair[:, :, 1], ALU.min)
+                nc.scalar.activation(sg[:, part], mn[:, part], ACT.Sigmoid)
+            for part, pair in zip(parts, pairs):
+                nc.vector.tensor_tensor(mx[:, part], pair[:, :, 0], pair[:, :, 1], ALU.max)
+
+        def quantise(c, mx, sg):
+            n = CHUNKS[c]
+            if c == 0:
+                z_rows = keep.tile([P, PACK, n], BF16, name="z_rows")
                 for t in range(PACK):
                     part = slice(t * n, (t + 1) * n)
                     nc.vector.scalar_tensor_tensor(z_rows[:, t, :], mx[:, part], gs_sb[:, t : t + 1], sg[:, part], ALU.mult, ALU.mult)
                 z_grouped = keep.tile([P, PACK * n], BF16, name="z_grouped", tag="turn", align_bytes=64)
-                if c == 0:
-                    nc.vector.tensor_copy(z_grouped[:].rearrange("p (v t) -> p v t", t=PACK), z_rows[:].rearrange("p t v -> p v t"))
-                else:
-                    nc.scalar.copy(z_grouped[:].rearrange("p (v t) -> p v t", t=PACK), z_rows[:].rearrange("p t v -> p v t"))
+                nc.vector.tensor_copy(z_grouped[:].rearrange("p (v t) -> p v t", t=PACK), z_rows[:].rearrange("p t v -> p v t"))
             else:
-                gated = ring.tile([P, PACK * n], F32, name="gated")
-                nc.gpsimd.tensor_tensor(gated[:], mx, sg[:], ALU.mult)
+                gated = keep.tile([P, PACK * n], F32, name="gated", tag=f"gated{c}")
+                nc.gpsimd.tensor_tensor(gated[:], mx, sg, ALU.mult)
                 z_grouped = keep.tile([P, PACK * n], BF16, name="z_grouped", tag="turn", align_bytes=64)
                 nc.gpsimd.tensor_tensor(z_grouped[:].rearrange("p (v t) -> p v t", t=PACK), gated[:].rearrange("p (t v) -> p v t", t=PACK),
                                         gs_sb[:].unsqueeze(1).to_broadcast([P, n, PACK]), ALU.mult)
@@ -144,37 +150,60 @@ def tile_picked_candpgatesend_none_p_kernel(tc, x_words, x_scales, w1, gs, offs,
             nc.vector.quantize_mx(out=z_codes[:].bitcast(FP8X4), scales=z_scales[:], in_=z_grouped[:])
             return z_codes, z_scales
 
-        def multiply(z_codes, z_scales, v0, n):
-            rl = ring.tile([P, PACK, n], F32, name="rl")
+        def multiply(c, z_codes, z_scales):
+            v0, n = starts[c], CHUNKS[c]
             for t in range(PACK):
                 rows = slice(t * P, (t + 1) * P)
                 nc.tensor.matmul_mx(out=score[t][:, v0 : v0 + n], lhsT=xc_words[:, rows].bitcast(FP8X4), lhsT_scale=xc_scales[:, rows],
                                     rhs=z_codes[:].bitcast(FP8X4), rhs_scale=z_scales[:], start=True, stop=True)
-                nc.scalar.activation(rl[:, t, :], score[t][:, v0 : v0 + n], ACT.Relu, scale=0.0625)
-            return rl
+                if (c, t) not in HELD:
+                    rectify(c, t, f"rl{c}{t}")
 
-        def send(rl, v0, n, last):
-            places = n2_sb[:, v0 // STRIPE : (v0 + n) // STRIPE]
-            for t in range(PACK):
-                nc.vector.tensor_copy(ds[t][:].indirect(places), rl[:, t, :])
-                if last:
-                    result = keep.tile([P, V], F32, name=f"result{t}")
-                    if t < 2 and True:
-                        less = keep.tile([P, V], F32, name=f"less{t}")
-                        nc.scalar.activation(less[:], score[t][:], ACT.Copy, scale=-0.03125)
-                        nc.gpsimd.tensor_tensor(result[:], less[:], ds[t][:], ALU.add)
-                    else:
-                        nc.vector.scalar_tensor_tensor(result[:], score[t][:], -0.03125, ds[t][:], ALU.mult, ALU.add)
-                    nc.sync.dma_start(out_rows[:, t, :], result[:])
+        def rectify(c, t, tag):
+            v0, n = starts[c], CHUNKS[c]
+            rl[c, t] = keep.tile([P, n], F32, name="rl", tag=tag)
+            nc.scalar.activation(rl[c, t][:], score[t][:, v0 : v0 + n], ACT.Relu, scale=0.0625)
 
-        starts = [sum(CHUNKS[:c]) for c in range(len(CHUNKS))]
-        last = len(CHUNKS) - 1
-        fetched = fetch(0, starts[0], CHUNKS[0])
-        gated_pair = gate(0, fetched, CHUNKS[0])
-        for c, n in enumerate(CHUNKS):
-            codes = quantise(c, *gated_pair, n)
-            rl = multiply(*codes, starts[c], n)
+        def send(c, t):
+            v0, n = starts[c], CHUNKS[c]
+            nc.vector.tensor_copy(ds[t][:].indirect(n2_sb[:, v0 // STRIPE : (v0 + n) // STRIPE]), rl[c, t][:])
+
+        def finish(t):
+            result = keep.tile([P, V], F32, name=f"result{t}")
+            if t < 2:
+                less = keep.tile([P, V], F32, name=f"less{t}")
+                nc.scalar.activation(less[:], score[t][:], ACT.Copy, scale=-0.03125)
+                nc.gpsimd.tensor_tensor(result[:], less[:], ds[t][:], ALU.add)
+                nc.sync.dma_start(out_rows[:, t, :], result[:])
+            else:
+                nc.vector.scalar_tensor_tensor(result[:], score[t][:], -0.03125, ds[t][:], ALU.mult, ALU.add)
+                nc.scalar.dma_start(out_rows[:, t, :], result[:])
+
+        halves, whole = ((0, 1), (2, 3)), ((0, 1, 2, 3),)
+        mn, mx, sg = gate_tiles(0)
+        project(halves[0])
+        early = fetch(0, halves[0])
+        project(halves[1])
+        gate(0, halves, [early, fetch(0, halves[1])], mn, mx, sg)
+
+        score = [psum.tile([P, V], F32, name=f"score{t}", tag=f"bank0{t}") for t in range(PACK)]
+        rl = {}
+        ds = [keep.tile([P, V], F32, name=f"ds{t}") for t in range(PACK)]
+        out_rows = out.rearrange("(p t) v -> p t v", t=PACK)
+        for c in range(len(CHUNKS)):
+            codes = quantise(c, mx, sg)
+            late = [t for t in range(PACK) if (c - 1, t) in HELD]
+            for t in late:
+                rectify(c - 1, t, f"gated{c}")
+            multiply(c, *codes)
             if c < last:
-                fetched = fetch(c + 1, starts[c + 1], CHUNKS[c + 1])
-                gated_pair = gate(c + 1, fetched, CHUNKS[c + 1])
-            send(rl, starts[c], n, c == last)
+                mn, mx, sg = gate_tiles(c + 1)
+                groups = halves if c == 0 else whole
+                gate(c + 1, groups, [fetch(c + 1, group) for group in groups], mn, mx, sg)
+            for t in late:
+                send(c - 1, t)
+            for t in range(PACK):
+                if (c, t) not in HELD:
+                    send(c, t)
+                if c == last:
+                    finish(t)

@@ -19,7 +19,7 @@ P = 128
 PACK = 4
 BANK = 512
 STRIPE = 16
-W_PIECES = ((0, 128), (128, 320), (320, 512))
+W_PIECES = ((0, 128), (128, 320), (320, 448), (448, 512))
 HELD = ((1, 3), (2, 3))
 CHUNKS = (128, 128, 128, 128)
 
@@ -30,6 +30,7 @@ def tile_picked_candpgatesend_none_p_kernel(tc, x_words, x_scales, w1, gs, offs,
         lists = ctx.enter_context(tc.tile_pool(name="lists", bufs=1))
         keep = ctx.enter_context(tc.tile_pool(name="keep", bufs=1))
         ring = ctx.enter_context(tc.tile_pool(name="ring", bufs=2))
+        reuse = ctx.enter_context(tc.tile_pool(name="reuse", bufs=1))
         psum = ctx.enter_context(tc.psum_pool(name="psum", bufs=1))
 
         offs_sb = lists.tile([P, S // STRIPE], U16, name="offs_sb")
@@ -52,9 +53,9 @@ def tile_picked_candpgatesend_none_p_kernel(tc, x_words, x_scales, w1, gs, offs,
         nc.sync.dma_start(w_raw[0][:], w_rows[:, :, W_PIECES[0][0] : W_PIECES[0][1]])
         for q in range(4):
             nc.sync.dma_start(scale_table[32 * q : 32 * q + 4, :].bitcast(I32), x_scales[0, 4 * q : 4 * q + 4, :].bitcast(I32))
+        nc.sync.dma_start(word_table[:], x_words[0].rearrange("p n t -> p (n t)").bitcast(I32))
         for piece, (lo, hi) in list(zip(w_raw, W_PIECES))[1:]:
             nc.sync.dma_start(piece[:], w_rows[:, :, lo:hi])
-        nc.sync.dma_start(word_table[:], x_words[0].rearrange("p n t -> p (n t)").bitcast(I32))
         nc.sync.dma_start(n1_sb[:], n1)
         gs_sb = keep.tile([P, PACK], F32, name="gs_sb")
         nc.sync.dma_start(gs_sb[:], gs.rearrange("(p t) o -> p (t o)", t=PACK))
@@ -62,23 +63,28 @@ def tile_picked_candpgatesend_none_p_kernel(tc, x_words, x_scales, w1, gs, offs,
 
         xq_scales = keep.tile([P, S], U8, name="xq_scales", align_bytes=64)
         nc.vector.tensor_copy(xq_scales[:], scale_table[:].indirect(offs_sb[:]))
-        xc_scales = keep.tile([P, C], U8, name="xc_scales", align_bytes=64)
-        nc.vector.tensor_copy(xc_scales[:].rearrange("p (t m) -> p m t", t=PACK), scale_table[:].indirect(cand_sb[:]))
-
-        w_grouped = keep.tile([P, PACK * H], BF16, name="w_grouped", tag="first", align_bytes=64)
-        w_dst = w_grouped[:].rearrange("p (t m j) -> p m t j", t=PACK, j=PACK)
-        for piece, (lo, hi) in zip(w_raw, W_PIECES):
-            nc.scalar.copy(w_dst[:, lo // PACK : hi // PACK], piece[:].rearrange("p j (m t) -> p m t j", t=PACK))
-        w_codes = keep.tile([P, H], U32, name="w_codes", align_bytes=64)
-        w_scales = keep.tile([P, H], U8, name="w_scales", align_bytes=64)
-        nc.vector.quantize_mx(out=w_codes[:].bitcast(FP8X4), scales=w_scales[:], in_=w_grouped[:])
-
         xq_words = []
         for h in range(S // BANK):
-            picked = keep.tile([P, BANK], U32, name=f"xq_words{h}", tag=("first", "second")[h], align_bytes=64)
+            picked = keep.tile([P, BANK], U32, name=f"xq_words{h}", align_bytes=64)
             nc.vector.tensor_copy(picked[:], word_table[:].bitcast(U32).indirect(offs_sb[:, h * BANK // STRIPE : (h + 1) * BANK // STRIPE]))
             xq_words.append(picked)
-        xc_words = keep.tile([P, C], U32, name="xc_words", align_bytes=64)
+
+        w_grouped = reuse.tile([P, PACK * H], BF16, name="w_grouped", align_bytes=64, offset=0)
+        w_dst = w_grouped[:].rearrange("p (t m j) -> p m t j", t=PACK, j=PACK)
+        for piece, (lo, hi) in zip(w_raw, W_PIECES):
+            src = piece[:].rearrange("p j (m t) -> p m t j", t=PACK)
+            if lo == W_PIECES[2][0]:
+                nc.gpsimd.tensor_scalar(w_dst[:, lo // PACK : hi // PACK], src, 1.0, 0.0, ALU.mult, ALU.add)
+            else:
+                nc.scalar.copy(w_dst[:, lo // PACK : hi // PACK], src)
+        w_codes = keep.tile([P, H], U32, name="w_codes", align_bytes=64)
+        w_scales = keep.tile([P, H], U8, name="w_scales", align_bytes=64)
+        for lo, hi in ((0, 128), (128, 256), (256, 512)):
+            nc.vector.quantize_mx(out=w_codes[:, lo:hi].bitcast(FP8X4), scales=w_scales[:, lo:hi], in_=w_grouped[:, PACK * lo : PACK * hi])
+
+        xc_scales = reuse.tile([P, C], U8, name="xc_scales", align_bytes=64, offset=0)
+        nc.vector.tensor_copy(xc_scales[:].rearrange("p (t m) -> p m t", t=PACK), scale_table[:].indirect(cand_sb[:]))
+        xc_words = reuse.tile([P, C], U32, name="xc_words", align_bytes=64, offset=1024)
         nc.vector.tensor_copy(xc_words[:].rearrange("p (t m) -> p m t", t=PACK), word_table[:].bitcast(U32).indirect(cand_sb[:]))
 
         y = [keep.tile([P, S], F32, name=f"y{t}") for t in range(PACK)]
@@ -86,8 +92,8 @@ def tile_picked_candpgatesend_none_p_kernel(tc, x_words, x_scales, w1, gs, offs,
         last = len(CHUNKS) - 1
 
         def project(pair):
-            for h in range(S // BANK):
-                for t in pair:
+            for t in pair:
+                for h in range(S // BANK):
                     cols = slice(h * BANK, (h + 1) * BANK)
                     rows = slice(t * P, (t + 1) * P)
                     acc = psum.tile([P, BANK], F32, name=f"y_acc{h}{t}", tag=f"bank{h}{t}")

from contextlib import ExitStack

import concourse.mybir as mybir

K, T, S, V, H, C = 512, 2048, 1024, 512, 512, 512
FLOPS = 2 * K * H * S + 2 * K * C * V

F32 = mybir.dt.float32
BF16 = mybir.dt.bfloat16
I32 = mybir.dt.int32
U32 = mybir.dt.uint32
U16 = mybir.dt.uint16
U8 = mybir.dt.uint8
FP8X4 = mybir.dt.float8_e4m3fn_x4
ACT = mybir.ActivationFunctionType
ALU = mybir.AluOpType

P = 128
PACK = 4
BANK = 512
STRIPE = 16
W_PIECES = ((0, 128), (128, 320), (320, 448), (448, 512))
HELD = ((1, 3), (2, 3))
CHUNKS = (128, 128, 128, 128)


def tile_picked_candpgatesend_none_p_kernel(tc, x_words, x_scales, w1, gs, offs, n1, cand, n2, out):
    nc = tc.nc
    with ExitStack() as ctx:
        lists = ctx.enter_context(tc.tile_pool(name="lists", bufs=1))
        keep = ctx.enter_context(tc.tile_pool(name="keep", bufs=1))
        ring = ctx.enter_context(tc.tile_pool(name="ring", bufs=2))
        reuse = ctx.enter_context(tc.tile_pool(name="reuse", bufs=1))
        psum = ctx.enter_context(tc.psum_pool(name="psum", bufs=1))

        offs_sb = lists.tile([P, S // STRIPE], U16, name="offs_sb")
        cand_sb = lists.tile([P, C // STRIPE], U16, name="cand_sb")
        n1_sb = lists.tile([P, S // STRIPE], U16, name="n1_sb")
        n2_sb = lists.tile([P, V // STRIPE], U16, name="n2_sb")

        scale_table = keep.tile([P, T], U8, name="scale_table", align_bytes=64)
        word_table = keep.tile([P, T], I32, name="word_table", align_bytes=64)
        nc.vector.memset(scale_table[:].bitcast(I32), 0)
        warm_in = keep.tile([P, 8], F32, name="warm_in")
        warm_out = keep.tile([P, 8], F32, name="warm_out")
        nc.gpsimd.memset(warm_in[:], 0.0)
        nc.scalar.activation(warm_out[:], warm_in[:], ACT.Sigmoid)

        nc.sync.dma_start(offs_sb[:], offs)
        nc.sync.dma_start(cand_sb[:], cand)
        w_rows = w1.rearrange("(p j) c -> p j c", j=PACK)
        w_raw = [keep.tile([P, PACK, hi - lo], F32, name=f"w_raw{lo}") for lo, hi in W_PIECES]
        nc.sync.dma_start(w_raw[0][:], w_rows[:, :, W_PIECES[0][0] : W_PIECES[0][1]])
        for q in range(4):
            nc.sync.dma_start(scale_table[32 * q : 32 * q + 4, :].bitcast(I32), x_scales[0, 4 * q : 4 * q + 4, :].bitcast(I32))
        nc.sync.dma_start(word_table[:], x_words[0].rearrange("p n t -> p (n t)").bitcast(I32))
        for piece, (lo, hi) in list(zip(w_raw, W_PIECES))[1:]:
            nc.sync.dma_start(piece[:], w_rows[:, :, lo:hi])
        nc.sync.dma_start(n1_sb[:], n1)
        gs_sb = keep.tile([P, PACK], F32, name="gs_sb")
        nc.sync.dma_start(gs_sb[:], gs.rearrange("(p t) o -> p (t o)", t=PACK))
        nc.sync.dma_start(n2_sb[:], n2)

        xq_scales = keep.tile([P, S], U8, name="xq_scales", align_bytes=64)
        nc.vector.tensor_copy(xq_scales[:], scale_table[:].indirect(offs_sb[:]))
        xq_words = []
        for h in range(S // BANK):
            picked = keep.tile([P, BANK], U32, name=f"xq_words{h}", align_bytes=64)
            nc.vector.tensor_copy(picked[:], word_table[:].bitcast(U32).indirect(offs_sb[:, h * BANK // STRIPE : (h + 1) * BANK // STRIPE]))
            xq_words.append(picked)

        w_grouped = reuse.tile([P, PACK * H], BF16, name="w_grouped", align_bytes=64, offset=0)
        w_dst = w_grouped[:].rearrange("p (t m j) -> p m t j", t=PACK, j=PACK)
        for piece, (lo, hi) in zip(w_raw, W_PIECES):
            src = piece[:].rearrange("p j (m t) -> p m t j", t=PACK)
            if lo == W_PIECES[2][0]:
                nc.gpsimd.tensor_scalar(w_dst[:, lo // PACK : hi // PACK], src, 1.0, 0.0, ALU.mult, ALU.add)
            else:
                nc.scalar.copy(w_dst[:, lo // PACK : hi // PACK], src)
        w_codes = keep.tile([P, H], U32, name="w_codes", align_bytes=64)
        w_scales = keep.tile([P, H], U8, name="w_scales", align_bytes=64)
        for lo, hi in ((0, 128), (128, 256), (256, 512)):
            nc.vector.quantize_mx(out=w_codes[:, lo:hi].bitcast(FP8X4), scales=w_scales[:, lo:hi], in_=w_grouped[:, PACK * lo : PACK * hi])

        xc_scales = reuse.tile([P, C], U8, name="xc_scales", align_bytes=64, offset=0)
        nc.vector.tensor_copy(xc_scales[:].rearrange("p (t m) -> p m t", t=PACK), scale_table[:].indirect(cand_sb[:]))
        xc_words = reuse.tile([P, C], U32, name="xc_words", align_bytes=64, offset=1024)
        nc.vector.tensor_copy(xc_words[:].rearrange("p (t m) -> p m t", t=PACK), word_table[:].bitcast(U32).indirect(cand_sb[:]))

        y = [keep.tile([P, S], F32, name=f"y{t}") for t in range(PACK)]
        starts = [sum(CHUNKS[:c]) for c in range(len(CHUNKS))]
        last = len(CHUNKS) - 1

        def project(pair):
            for t in pair:
                for h in range(S // BANK):
                    cols = slice(h * BANK, (h + 1) * BANK)
                    rows = slice(t * P, (t + 1) * P)
                    acc = psum.tile([P, BANK], F32, name=f"y_acc{h}{t}", tag=f"bank{h}{t}")
                    nc.tensor.matmul_mx(out=acc[:], lhsT=w_codes[:, rows].bitcast(FP8X4), lhsT_scale=w_scales[:, rows],
                                        rhs=xq_words[h][:].bitcast(FP8X4), rhs_scale=xq_scales[:, cols], start=True, stop=True)
                    if pair[0] == 2 and h == 0:
                        nc.vector.tensor_copy(y[t][:, cols], acc[:])
                    else:
                        nc.scalar.copy(y[t][:, cols], acc[:])

        def fetch(c, group):
            v0, n = starts[c], CHUNKS[c]
            ln = keep.tile([P, len(group), 2 * n], F32, name="ln", tag="mn" if c == 1 and group[0] == 0 else f"ln{group[-1]}")
            picks = n1_sb[:, 2 * v0 // STRIPE : 2 * (v0 + n) // STRIPE]
            for i, t in enumerate(group):
                if c == 0 and i == 0:
                    nc.vector.tensor_copy(ln[:, i, :], y[t][:].indirect(picks))
                else:
                    nc.scalar.activation(ln[:, i, :], y[t][:].indirect(picks), ACT.Copy)
            return ln

        def gate_tiles(c):
            n = CHUNKS[c]
            if c == 1:
                both = keep.tile([P, 2 * PACK * n], F32, name="both", tag="turn", align_bytes=64)
                mn, mx = both[:, : PACK * n], both[:, PACK * n :]
            else:
                mn = keep.tile([P, PACK * n], F32, name="mn")[:]
                mx = keep.tile([P, PACK * n], F32, name="mx", tag="turn", align_bytes=64)[:]
            sg = ring.tile([P, PACK * n], F32, name="sg")
            return mn, mx, sg[:]

        def gate(c, groups, fetched, mn, mx, sg):
            n = CHUNKS[c]
            parts = [slice(group[0] * n, (group[-1] + 1) * n) for group in groups]
            pairs = [ln[:].rearrange("p t (v e) -> p (t v) e", e=2) for ln in fetched]
            for part, pair in zip(parts, pairs):
                nc.vector.tensor_tensor(mn[:, part], pair[:, :, 0], pair[:, :, 1], ALU.min)
                nc.scalar.activation(sg[:, part], mn[:, part], ACT.Sigmoid)
            for part, pair in zip(parts, pairs):
                nc.vector.tensor_tensor(mx[:, part], pair[:, :, 0], pair[:, :, 1], ALU.max)

        def quantise(c, mx, sg):
            n = CHUNKS[c]
            if c == 0:
                z_rows = keep.tile([P, PACK, n], BF16, name="z_rows")
                for t in range(PACK):
                    part = slice(t * n, (t + 1) * n)
                    nc.vector.scalar_tensor_tensor(z_rows[:, t, :], mx[:, part], gs_sb[:, t : t + 1], sg[:, part], ALU.mult, ALU.mult)
                z_grouped = keep.tile([P, PACK * n], BF16, name="z_grouped", tag="turn", align_bytes=64)
                nc.vector.tensor_copy(z_grouped[:].rearrange("p (v t) -> p v t", t=PACK), z_rows[:].rearrange("p t v -> p v t"))
            else:
                gated = keep.tile([P, PACK * n], F32, name="gated", tag=f"gated{c}")
                nc.gpsimd.tensor_tensor(gated[:], mx, sg, ALU.mult)
                z_grouped = keep.tile([P, PACK * n], BF16, name="z_grouped", tag="turn", align_bytes=64)
                nc.gpsimd.tensor_tensor(z_grouped[:].rearrange("p (v t) -> p v t", t=PACK), gated[:].rearrange("p (t v) -> p v t", t=PACK),
                                        gs_sb[:].unsqueeze(1).to_broadcast([P, n, PACK]), ALU.mult)
            z_codes = ring.tile([P, n], U32, name="z_codes", align_bytes=64)
            z_scales = ring.tile([P, n], U8, name="z_scales", align_bytes=64)
            nc.vector.quantize_mx(out=z_codes[:].bitcast(FP8X4), scales=z_scales[:], in_=z_grouped[:])
            return z_codes, z_scales

        def multiply(c, z_codes, z_scales):
            v0, n = starts[c], CHUNKS[c]
            for t in range(PACK):
                rows = slice(t * P, (t + 1) * P)
                nc.tensor.matmul_mx(out=score[t][:, v0 : v0 + n], lhsT=xc_words[:, rows].bitcast(FP8X4), lhsT_scale=xc_scales[:, rows],
                                    rhs=z_codes[:].bitcast(FP8X4), rhs_scale=z_scales[:], start=True, stop=True)
                if (c, t) not in HELD:
                    rectify(c, t, f"rl{c}{t}")

        def rectify(c, t, tag):
            v0, n = starts[c], CHUNKS[c]
            rl[c, t] = keep.tile([P, n], F32, name="rl", tag=tag)
            nc.scalar.activation(rl[c, t][:], score[t][:, v0 : v0 + n], ACT.Relu, scale=0.0625)

        def send(c, t):
            v0, n = starts[c], CHUNKS[c]
            nc.vector.tensor_copy(ds[t][:].indirect(n2_sb[:, v0 // STRIPE : (v0 + n) // STRIPE]), rl[c, t][:])

        def finish(t):
            result = keep.tile([P, V], F32, name=f"result{t}")
            if t < 2:
                less = keep.tile([P, V], F32, name=f"less{t}")
                nc.scalar.activation(less[:], score[t][:], ACT.Copy, scale=-0.03125)
                nc.gpsimd.tensor_tensor(result[:], less[:], ds[t][:], ALU.add)
                nc.sync.dma_start(out_rows[:, t, :], result[:])
            else:
                nc.vector.scalar_tensor_tensor(result[:], score[t][:], -0.03125, ds[t][:], ALU.mult, ALU.add)
                nc.scalar.dma_start(out_rows[:, t, :], result[:])

        halves, whole = ((0, 1), (2, 3)), ((0, 1, 2, 3),)
        mn, mx, sg = gate_tiles(0)
        project(halves[0])
        early = fetch(0, halves[0])
        project(halves[1])
        gate(0, halves, [early, fetch(0, halves[1])], mn, mx, sg)

        score = [psum.tile([P, V], F32, name=f"score{t}", tag=f"bank0{t}") for t in range(PACK)]
        rl = {}
        ds = [keep.tile([P, V], F32, name=f"ds{t}") for t in range(PACK)]
        out_rows = out.rearrange("(p t) v -> p t v", t=PACK)
        for c in range(len(CHUNKS)):
            codes = quantise(c, mx, sg)
            late = [t for t in range(PACK) if (c - 1, t) in HELD]
            for t in late:
                rectify(c - 1, t, f"gated{c}")
            multiply(c, *codes)
            if c < last:
                mn, mx, sg = gate_tiles(c + 1)
                groups = halves if c == 0 else whole
                gate(c + 1, groups, [fetch(c + 1, group) for group in groups], mn, mx, sg)
            for t in late:
                send(c - 1, t)
            for t in range(PACK):
                if (c, t) not in HELD:
                    send(c, t)
                if c == last:
                    finish(t)
